import numpy as np
import ml_dtypes


def mxq(x, axis, fmt="e4m3"):
    dtype, down = {"e4m3": (ml_dtypes.float8_e4m3fn, 7), "e5m2": (ml_dtypes.float8_e5m2, 14)}[fmt]
    v = np.moveaxis(np.asarray(x, np.float32).astype(ml_dtypes.bfloat16).astype(np.float64), axis, -1)
    blocks = v.reshape(v.shape[:-1] + (-1, 32))
    amax = np.abs(blocks).max(-1, keepdims=True)
    byte = np.maximum(np.where(amax > 0, np.frexp(amax)[1] - 1 + 127, 0) - down, 1)
    scale = np.exp2(byte - 127.0)
    codes = (blocks / scale).astype(np.float32).astype(dtype).astype(np.float64)
    return np.moveaxis((codes * scale).reshape(v.shape), -1, axis)


WIDE = False


def mx_kscale(k):
    if not WIDE:
        return np.ones(k)
    levels = np.array([10, -10, 5, -5, 0])
    if k % 512:
        return np.exp2(np.random.permutation(np.resize(levels, k // 32))).repeat(32)
    a = np.empty((k // 512, 16))
    for p in range(k // 512):
        a[p, :8] = np.random.permutation(np.resize(levels, 8))
        for g in range(8):
            far = levels[np.abs(levels - a[p, g]) >= 10]
            a[p, g + 8] = far[np.random.randint(len(far))]
    return np.exp2(a.ravel()).repeat(32)


def f64(x):
    return np.asarray(x).astype(np.float64)


def striped(idx):
    return np.tile(idx.reshape(-1, 16).T, (8, 1)).astype(np.uint16)


def unstriped(offs):
    return offs[:16].T.reshape(-1).astype(np.int64)


def striped8(idx):
    return np.concatenate([x.reshape(-1, 16).T for x in idx]).astype(np.uint16)


def runs(offs, k):
    lists = np.stack([offs[16 * r : 16 * r + 16].T.reshape(-1) for r in range(8)]).astype(np.int64)
    return lists[np.arange(k) % 512 // 64]


def pack_weight(w):
    k, n = w.shape
    w = f64(np.asarray(w, np.float32).astype(ml_dtypes.bfloat16)).reshape(k // 32, 32, n)
    amax = np.abs(w).max(1)
    byte = np.clip(np.where(amax > 0, np.frexp(amax)[1] - 1 + 127 - 7, 1), 1, 254)
    scaled = (w * np.exp2(127.0 - byte)[:, None, :]).reshape(k, n).astype(np.float32)
    words = np.ascontiguousarray(scaled.reshape(k // 512, 128, 4, n).transpose(0, 1, 3, 2)).astype(ml_dtypes.float8_e4m3fn).view(np.uint8)
    return words, np.ascontiguousarray(byte.astype(np.uint8).reshape(k // 512, 16, n))


def unpack_weight(words, scales):
    g, p, n, _ = words.shape
    vals = np.ascontiguousarray(words).view(ml_dtypes.float8_e4m3fn).astype(np.float64) * np.repeat(np.exp2(scales.astype(np.float64) - 127.0), 8, axis=1)[..., None]
    return vals.transpose(0, 1, 3, 2).reshape(g * 512, n)


E2M1 = np.array([0.0, 0.5, 1.0, 1.5, 2.0, 3.0, 4.0, 6.0, -0.0, -0.5, -1.0, -1.5, -2.0, -3.0, -4.0, -6.0])


def pack_fp4(w):
    k, n = w.shape
    w = f64(np.asarray(w, np.float32).astype(ml_dtypes.bfloat16)).reshape(k // 32, 32, n)
    amax = np.abs(w).max(1)
    mant, ex = np.frexp(amax / 6.0)
    byte = np.clip(np.where(amax > 0, np.where(mant > 0.5, ex, ex - 1) + 127, 1), 1, 254)
    scaled = (w * np.exp2(127.0 - byte)[:, None, :]).reshape(k, n).astype(np.float32)
    c = np.ascontiguousarray(scaled.reshape(k // 512, 128, 4, n).transpose(0, 1, 3, 2)).astype(ml_dtypes.float4_e2m1fn).view(np.uint8) & 0xF
    words = (c[..., 0::2] | (c[..., 1::2] << 4)).reshape(k // 512, 128, 2 * n)
    return np.ascontiguousarray(words), np.ascontiguousarray(byte.astype(np.uint8).reshape(k // 512, 16, n))


def unpack_fp4(words, scales):
    g, _, n = scales.shape
    words = np.ascontiguousarray(words).reshape(g, 128, n, 2)
    nib = np.empty((g, 128, n, 4), np.uint8)
    nib[..., 0::2] = words & 0xF
    nib[..., 1::2] = words >> 4
    vals = E2M1[nib] * np.repeat(np.exp2(scales.astype(np.float64) - 127.0), 8, axis=1)[..., None]
    return vals.transpose(0, 1, 3, 2).reshape(g * 512, n)


def relu(v):
    return np.maximum(v, 0.0)


def sigmoid(v):
    return 1.0 / (1.0 + np.exp(-np.maximum(v, -700.0)))

def planes(y):
    n, m = y.shape
    v = y.astype(np.float32).astype(ml_dtypes.bfloat16).astype(np.float64).reshape(n // 32, 32, m)
    top = np.abs(v).max(1)
    byte = np.clip(np.where(top > 0, np.frexp(top)[1] - 1 + 127 - 7, 1), 1, 254)
    codes = (v * np.exp2(127.0 - byte)[:, None, :]).reshape(n, m).astype(np.float32).astype(ml_dtypes.float8_e4m3fn).view(np.uint8)
    words = codes.reshape(n // 512, 128, 4, m).transpose(0, 1, 3, 2)
    return np.ascontiguousarray(words), np.ascontiguousarray(byte.astype(np.uint8).reshape(n // 512, 16, m))


K, T, S, N, H = 512, 2048, 512, 512, 512


def setup_inputs():
    n = np.random.standard_normal
    s = mx_kscale(K)[:, None]
    u = mx_kscale(H)
    packed_xT = pack_weight(n((K, T)) * s)
    packed_w1 = pack_fp4(n((K, H)) / np.sqrt(K) / s)
    packed_w2 = pack_fp4(n((K, H)) / np.sqrt(K) / s)
    packed_w3 = pack_fp4(n((H, H)) / np.sqrt(H) / u[:, None])
    packed_w4 = pack_fp4(n((H, N)) / np.sqrt(H) / u[:, None])
    return {
        "x_words": packed_xT[0],
        "x_scales": packed_xT[1],
        "w1_words": packed_w1[0],
        "w1_scales": packed_w1[1],
        "w2_words": packed_w2[0],
        "w2_scales": packed_w2[1],
        "gn": (np.random.uniform(0.5, 1.5, (H, 1)) * u[:, None]).astype(np.float32),
        "w3_words": packed_w3[0],
        "w3_scales": packed_w3[1],
        "res": n((N, S)).astype(np.float32),
        "w4_words": packed_w4[0],
        "w4_scales": packed_w4[1],
        "offs": striped(np.random.permutation(T)[:S]),
        "two": striped(np.random.permutation(T)[:S]),
        "in1": striped8(np.stack([np.random.permutation(S) for _ in range(8)])),
        "in2": striped8(np.stack([np.random.permutation(S) for _ in range(8)])),
        "mv": striped8(np.stack([np.random.permutation(S) for _ in range(8)])),
    }


def reference(x_words, x_scales, w1_words, w1_scales, w2_words, w2_scales, gn, w3_words, w3_scales, res, w4_words, w4_scales, offs, two, in1, in2, mv):
    xq = unpack_weight(x_words, x_scales)[:, unstriped(offs)]
    y = unpack_fp4(w1_words, w1_scales).T @ xq
    x_two = unpack_weight(x_words, x_scales)[:, unstriped(two)]
    c = sigmoid(unpack_fp4(w2_words, w2_scales).T @ x_two)
    pu = np.minimum(relu(y), c)
    z = f64(gn) * (y - pu + pu[np.arange(H)[:, None], runs(in1, H)] + -0.5 * (pu[np.arange(H)[:, None], runs(in2, H)]))
    h = np.tanh(unpack_fp4(w3_words, w3_scales).T @ mxq(z, 0, "e4m3"))
    z2 = f64(gn) * (h[np.arange(H)[:, None], runs(mv, H)])
    out_0 = f64(res) + (unpack_fp4(w4_words, w4_scales).T @ mxq(z2, 0, "e4m3"))
    return (out_0,) + planes(out_0)

@@ -1,0 +1,285 @@
+from contextlib import ExitStack
+
+import concourse.mybir as mybir
+
+K, T, S, N, H = 512, 2048, 512, 512, 512
+FLOPS = 4 * 2 * 512 * 512 * 512
+
+F32 = mybir.dt.float32
+BF16 = mybir.dt.bfloat16
+I32 = mybir.dt.int32
+U32 = mybir.dt.uint32
+U16 = mybir.dt.uint16
+U8 = mybir.dt.uint8
+FP8X4 = mybir.dt.float8_e4m3fn_x4
+FP4X4 = mybir.dt.float4_e2m1fn_x4
+ALU = mybir.AluOpType
+ACT = mybir.ActivationFunctionType
+
+P = 128
+PACK = 4
+MID_CHUNKS = [(0, 256), (256, 256)]
+END_CHUNKS = [(0, 128), (128, 128), (256, 128), (384, 128)]
+PUSH_ENG = "S"
+GAIN_ON_V = [4,2]
+GOT_FIRST = True
+HOLD_B = True
+HOLD_Z = True
+HOLD_Z2 = 1
+MOVE_ON_V = [4, 0, 0, 0]
+ROUND_ON_V = [0, 0, 0, 1]
+
+
+def tile_picked_pushflow_none_po_kernel(tc, x_words, x_scales, w1_words, w1_scales, w2_words, w2_scales, gn, w3_words, w3_scales, res, w4_words, w4_scales, offs, two, in1, in2, mv, out_0, out_1, out_2):
+    nc = tc.nc
+    with ExitStack() as ctx:
+        lists = ctx.enter_context(tc.tile_pool(name="lists", bufs=1))
+        sb = ctx.enter_context(tc.tile_pool(name="sb", bufs=1))
+        psum = ctx.enter_context(tc.psum_pool(name="psum", bufs=1))
+
+        def load_list(name, src):
+            tl = lists.tile([P, S // 16], U16, name=name)
+            nc.sync.dma_start(tl[:], src)
+            return tl
+
+        def load_scale_rows(queue, name, src):
+            width = src.shape[2]
+            tl = sb.tile([P, width], U8, name=name, align_bytes=64)
+            for q in range(4):
+                queue[q].dma_start(tl[32 * q : 32 * q + 32, :].bitcast(I32), src[0, 4 * q : 4 * q + 4, :].bitcast(I32).partition_broadcast(8))
+            return tl
+
+        def load_words(queue, name, src):
+            tl = sb.tile([P, 2 * H], U8, name=name, align_bytes=64)
+            queue.dma_start(tl[:].bitcast(I32), src[0].bitcast(I32))
+            return tl
+
+        def deal_words(name, raw):
+            tl = sb.tile([P, 2 * H], U8, name=name, align_bytes=64)
+            nc.scalar.copy(tl[:].bitcast(U16).rearrange("p (t m) -> p m t", t=PACK), raw[:].bitcast(U16).rearrange("p (m t) -> p m t", t=PACK))
+            return tl
+
+        def deal_word_bytes(name, raw):
+            tl = sb.tile([P, 2 * H], U8, name=name, align_bytes=64)
+            nc.vector.tensor_copy(tl[:].rearrange("p (t m b) -> p t m b", t=PACK, b=2), raw[:].rearrange("p (m t b) -> p t m b", t=PACK, b=2))
+            return tl
+
+        def deal_scales(engine, name, raw):
+            tl = sb.tile([P, H], U8, name=name, align_bytes=64)
+            engine.tensor_copy(tl[:].rearrange("p (t m) -> p t m", t=PACK), raw[:].rearrange("p (m t) -> p t m", t=PACK))
+            return tl
+
+        def bank(b, parts, width):
+            return psum.tile([P, parts, width], F32, name="bank%d" % b, tag="bank%d" % b)
+
+        def product(out, words, scales, t, rhs, rhs_scale):
+            nc.tensor.matmul_mx(out=out, lhsT=words[:, 2 * P * t : 2 * P * (t + 1)].bitcast(FP4X4), lhsT_scale=scales[:, P * t : P * (t + 1)],
+                                rhs=rhs.bitcast(FP8X4), rhs_scale=rhs_scale, start=True, stop=True)
+
+        def by_lines(ap):
+            return ap.rearrange("p t (c i) -> p c t i", i=4)
+
+        def woven(ap):
+            return ap.rearrange("p (c i) t -> p c t i", i=4)
+
+        def cols(lst, n0, n):
+            return lst[:, n0 // 16 : (n0 + n) // 16]
+
+        two_l = load_list("two_l", two)
+        xs = load_scale_rows([nc.scalar, nc.sync, nc.scalar, nc.scalar], "xs", x_scales)
+        offs_l = load_list("offs_l", offs)
+        xw = sb.tile([P, T], U32, name="xw", align_bytes=64)
+        nc.sync.dma_start(xw[:].bitcast(I32), x_words[0].rearrange("p n t -> p (n t)").bitcast(I32))
+        w2w_raw = load_words(nc.scalar, "w2w_raw", w2_words)
+        w1s_raw = load_scale_rows([nc.gpsimd] * 4, "w1s_raw", w1_scales)
+        w2s_raw = load_scale_rows([nc.scalar] * 4, "w2s_raw", w2_scales)
+        w1w_raw = load_words(nc.sync, "w1w_raw", w1_words)
+        w3w_raw = load_words(nc.sync, "w3w_raw", w3_words)
+        w4w_raw = load_words(nc.sync, "w4w_raw", w4_words)
+        gain = sb.tile([P, PACK], F32, name="gain")
+        nc.sync.dma_start(gain[:], gn.rearrange("(p t) o -> p (t o)", t=PACK))
+        in2_l = load_list("in2_l", in2)
+        in1_l = load_list("in1_l", in1)
+        w3s_raw = load_scale_rows([nc.sync] * 4, "w3s_raw", w3_scales)
+        w4s_raw = load_scale_rows([nc.sync] * 4, "w4s_raw", w4_scales)
+        mv_l = load_list("mv_l", mv)
+        res_sb = sb.tile([P, PACK, S], F32, name="res_sb")
+        nc.sync.dma_start(res_sb[:], res.rearrange("(p t) n -> p t n", t=PACK))
+
+        def pick(name, table, lst, dtype):
+            tl = sb.tile([P, S], dtype, name=name, align_bytes=64)
+            nc.vector.tensor_copy(tl[:], table[:].indirect(lst[:]))
+            return tl
+
+        two_s = pick("two_s", xs, two_l, U8)
+        offs_s = pick("offs_s", xs, offs_l, U8)
+        w2w = deal_words("w2w", w2w_raw)
+        w2s = deal_scales(nc.gpsimd, "w2s", w2s_raw)
+        two_w = pick("two_w", xw, two_l, U32)
+        w1w = deal_words("w1w", w1w_raw)
+        w1s = deal_scales(nc.gpsimd, "w1s", w1s_raw)
+        offs_w = pick("offs_w", xw, offs_l, U32)
+
+        cap, push = [], []
+        keep = sb.tile([P, PACK, S], F32, name="keep")
+
+        def capacity(t):
+            pre = bank(t, 1, S)
+            product(pre[:, 0, :], w2w, w2s, t, two_w[:], two_s[:])
+            c_t = sb.tile([P, S], F32, name="cap%d" % t)
+            nc.scalar.activation(c_t[:], pre[:, 0, :], ACT.Sigmoid)
+            cap.append(c_t)
+
+        ys = []
+
+        def excess(t):
+            y = bank(4 + t, 1, S)
+            product(y[:, 0, :], w1w, w1s, t, offs_w[:], offs_s[:])
+            pu = sb.tile([P, S], F32, name="pu%d" % t)
+            nc.vector.scalar_tensor_tensor(pu[:], y[:, 0, :], 0.0, cap[t][:], ALU.max, ALU.min)
+            pg = sb.tile([P, S], F32, name="push%d" % t)
+            if PUSH_ENG == "S":
+                nc.scalar.activation(pg[:], pu[:], ACT.Copy, scale=gain[:, t : t + 1])
+            elif PUSH_ENG == "V":
+                nc.vector.tensor_scalar(pg[:], pu[:], gain[:, t : t + 1], None, ALU.mult)
+            else:
+                nc.gpsimd.tensor_scalar(pg[:], pu[:], gain[:, t : t + 1], 0.0, ALU.mult, ALU.add)
+            push.append(pg)
+            ys.append(y)
+
+        def kept(t):
+            nc.vector.scalar_tensor_tensor(keep[:, t, :], ys[t][:, 0, :], gain[:, t : t + 1], push[t][:], ALU.mult, ALU.subtract)
+
+        capacity(0)
+        for t in range(PACK):
+            if t + 1 < PACK:
+                capacity(t + 1)
+            excess(t)
+            if t >= 1:
+                kept(t - 1)
+        kept(PACK - 1)
+
+        w3w = deal_word_bytes("w3w", w3w_raw)
+        w4w = deal_word_bytes("w4w", w4w_raw)
+        w3s = deal_scales(nc.gpsimd, "w3s", w3s_raw)
+        w4s = deal_scales(nc.gpsimd, "w4s", w4s_raw)
+        wide = END_CHUNKS[0][1]
+        gain_rows = []
+        for t in range(PACK if max(MOVE_ON_V) == PACK else 0):
+            gr = sb.tile([P, wide], F32, name="gain_row%d" % t)
+            nc.gpsimd.tensor_copy(gr[:], gain[:, t : t + 1].to_broadcast([P, wide]))
+            gain_rows.append(gr)
+
+        used = [0]
+
+        def next_bank():
+            used.append(0)
+            return (len(used) - 2) % 8
+
+        hid = [sb.tile([P, S], F32, name="hid%d" % t) for t in range(PACK)]
+        for ci, (n0, n) in enumerate(MID_CHUNKS):
+            lost = sb.tile([P, PACK, n], F32, name="lost%d" % ci, tag=("pu3" if ci == 1 and HOLD_B else "lost%d" % ci))
+            gained = sb.tile([P, PACK, n], F32, name="gained%d" % ci)
+            nv = GAIN_ON_V[ci]
+            if nv < PACK:
+                got = sb.tile([P, PACK - nv, n], F32, name="got%d" % ci, tag=("got" if HOLD_B else "got%d" % ci))
+            for t in range(PACK):
+                if not (GOT_FIRST and ci > 0):
+                    nc.scalar.activation(lost[:, t, :], push[t][:].indirect(cols(in2_l, n0, n)), ACT.Copy, scale=-0.5)
+                if t >= PACK - nv:
+                    nc.vector.tensor_tensor(gained[:, t, :], push[t][:].indirect(cols(in1_l, n0, n)), keep[:, t, n0 : n0 + n], ALU.add)
+                else:
+                    nc.scalar.activation(got[:, t, :], push[t][:].indirect(cols(in1_l, n0, n)), ACT.Copy)
+            for t in range(PACK):
+                if GOT_FIRST and ci > 0:
+                    nc.scalar.activation(lost[:, t, :], push[t][:].indirect(cols(in2_l, n0, n)), ACT.Copy, scale=-0.5)
+            if nv < PACK:
+                nc.vector.tensor_tensor(gained[:, : PACK - nv, :], got[:], keep[:, : PACK - nv, n0 : n0 + n], ALU.add)
+            z = sb.tile([P, n, PACK], BF16, name="z%d" % ci, tag="z" if HOLD_Z else "z%d" % ci, align_bytes=64)
+            nc.vector.tensor_tensor(woven(z[:]), by_lines(gained[:]), by_lines(lost[:]), ALU.add)
+            zw = sb.tile([P, n], U32, name="zw%d" % ci, align_bytes=64)
+            zs = sb.tile([P, n], U8, name="zs%d" % ci, align_bytes=64)
+            nc.vector.quantize_mx(out=zw[:].bitcast(FP8X4), scales=zs[:], in_=z[:].rearrange("p n t -> p (n t)"))
+            last_mid = ci == len(MID_CHUNKS) - 1
+            per = 1 if last_mid else S // n
+            for g0 in range(0, PACK, per):
+                acc = bank(next_bank(), per, n)
+                for u in range(per):
+                    product(acc[:, u, :], w3w, w3s, g0 + u, zw[:], zs[:])
+                for u in range(per):
+                    t = g0 + u
+                    nc.scalar.activation(hid[t][:, n0 : n0 + n], acc[:, u, :], ACT.Tanh)
+
+        out_rows = out_0.rearrange("(p t) n -> p t n", t=PACK)
+        out_words = out_1[0].rearrange("p n t -> p (n t)").bitcast(I32)
+        o_scales = sb.tile([P, S], U8, name="o_scales", align_bytes=64)
+        moved, zq = {}, {}
+
+        def fetch(ci):
+            n0, n = END_CHUNKS[ci]
+            mv_t = sb.tile([P, PACK, n], F32, name="moved%d" % ci, align_bytes=64)
+            for t in range(PACK):
+                if MOVE_ON_V[ci] == PACK:
+                    nc.vector.tensor_tensor(mv_t[:, t, :], hid[t][:].indirect(cols(mv_l, n0, n)), gain_rows[t][:, :n], ALU.mult)
+                elif t < MOVE_ON_V[ci]:
+                    nc.vector.tensor_copy(mv_t[:, t, :], hid[t][:].indirect(cols(mv_l, n0, n)))
+                else:
+                    nc.scalar.activation(mv_t[:, t, :], hid[t][:].indirect(cols(mv_l, n0, n)), ACT.Copy)
+            moved[ci] = mv_t
+
+        def quantise(ci):
+            n0, n = END_CHUNKS[ci]
+            z2 = sb.tile([P, n, PACK], BF16, name="z2_%d" % ci, tag="z2_%d" % (ci % HOLD_Z2), align_bytes=64)
+            if MOVE_ON_V[ci] == PACK:
+                nc.vector.tensor_copy(woven(z2[:]), by_lines(moved[ci][:]))
+            else:
+                spread = gain[:].unsqueeze(1).unsqueeze(3).to_broadcast([P, n // 4, PACK, 4])
+                nc.vector.tensor_tensor(woven(z2[:]), by_lines(moved[ci][:]), spread, ALU.mult)
+            zw = sb.tile([P, n], U32, name="z2w%d" % ci, align_bytes=64)
+            zs = sb.tile([P, n], U8, name="z2s%d" % ci, align_bytes=64)
+            nc.vector.quantize_mx(out=zw[:].bitcast(FP8X4), scales=zs[:], in_=z2[:].rearrange("p n t -> p (n t)"))
+            zq[ci] = (zw, zs)
+
+        accs, outs = {}, {}
+
+        def multiply(ci):
+            n0, n = END_CHUNKS[ci]
+            zw, zs = zq[ci]
+            per = S // n
+            accs[ci] = []
+            for g0 in range(0, PACK, per):
+                acc = bank(next_bank(), per, n)
+                for u in range(per):
+                    product(acc[:, u, :], w4w, w4s, g0 + u, zw[:], zs[:])
+                accs[ci].append((g0, per, acc))
+
+        def finish(ci):
+            n0, n = END_CHUNKS[ci]
+            o = sb.tile([P, PACK, n], F32, name="o%d" % ci)
+            for g0, per, acc in accs[ci]:
+                nc.vector.tensor_tensor(o[:, g0 : g0 + per, :], acc[:], res_sb[:, g0 : g0 + per, n0 : n0 + n], ALU.add)
+            nc.sync.dma_start(out_rows[:, :, n0 : n0 + n], o[:])
+            outs[ci] = o
+
+        def planes(ci):
+            n0, n = END_CHUNKS[ci]
+            o = outs[ci]
+            ob = sb.tile([P, n, PACK], BF16, name="ob%d" % ci, align_bytes=64)
+            if not ROUND_ON_V[ci]:
+                nc.scalar.copy(woven(ob[:]), by_lines(o[:]))
+            else:
+                nc.vector.tensor_copy(woven(ob[:]), by_lines(o[:]))
+            ow = sb.tile([P, n], U32, name="ow%d" % ci, align_bytes=64)
+            nc.vector.quantize_mx(out=ow[:].bitcast(FP8X4), scales=o_scales[:, n0 : n0 + n], in_=ob[:].rearrange("p n t -> p (n t)"))
+            nc.sync.dma_start(out_words[:, n0 : n0 + n], ow[:].bitcast(I32))
+
+        for ci in range(len(END_CHUNKS)):
+            fetch(ci)
+            quantise(ci)
+            multiply(ci)
+        for ci in range(len(END_CHUNKS)):
+            finish(ci)
+        for ci in range(len(END_CHUNKS)):
+            planes(ci)
+        for q in range(4):
+            (nc.scalar if q % 2 == 0 else nc.sync).dma_start(out_2[0, 4 * q : 4 * q + 4, :].bitcast(I32), o_scales[32 * q : 32 * q + 4, :].bitcast(I32))

@@ -23,6 +23,8 @@ END_CHUNKS = [(0, 128), (128, 128), (256, 128), (384, 128)]
 PUSH_ENG = "S"
 GAIN_ON_V = [4,2]
 GOT_FIRST = True
+C_BANKS = [0, 1, 2, 3]
+LAST_PER = 2
 HOLD_B = True
 HOLD_Z = True
 HOLD_Z2 = 1
@@ -44,7 +46,7 @@ def tile_picked_pushflow_none_po_kernel(tc, x_words, x_scales, w1_words, w1_scal
 
         def load_scale_rows(queue, name, src):
             width = src.shape[2]
-            tl = sb.tile([P, width], U8, name=name, align_bytes=64)
+            tl = sb.tile([P, width], U8, name=name, tag=name, align_bytes=64)
             for q in range(4):
                 queue[q].dma_start(tl[32 * q : 32 * q + 32, :].bitcast(I32), src[0, 4 * q : 4 * q + 4, :].bitcast(I32).partition_broadcast(8))
             return tl
@@ -59,13 +61,13 @@ def tile_picked_pushflow_none_po_kernel(tc, x_words, x_scales, w1_words, w1_scal
             nc.scalar.copy(tl[:].bitcast(U16).rearrange("p (t m) -> p m t", t=PACK), raw[:].bitcast(U16).rearrange("p (m t) -> p m t", t=PACK))
             return tl
 
-        def deal_word_bytes(name, raw):
-            tl = sb.tile([P, 2 * H], U8, name=name, align_bytes=64)
+        def deal_word_bytes(name, raw, tag):
+            tl = sb.tile([P, 2 * H], U8, name=name, tag=tag, align_bytes=64)
             nc.vector.tensor_copy(tl[:].rearrange("p (t m b) -> p t m b", t=PACK, b=2), raw[:].rearrange("p (m t b) -> p t m b", t=PACK, b=2))
             return tl
 
-        def deal_scales(engine, name, raw):
-            tl = sb.tile([P, H], U8, name=name, align_bytes=64)
+        def deal_scales(engine, name, raw, tag=None):
+            tl = sb.tile([P, H], U8, name=name, tag=tag or name, align_bytes=64)
             engine.tensor_copy(tl[:].rearrange("p (t m) -> p t m", t=PACK), raw[:].rearrange("p (m t) -> p t m", t=PACK))
             return tl
 
@@ -88,43 +90,43 @@ def tile_picked_pushflow_none_po_kernel(tc, x_words, x_scales, w1_words, w1_scal
         two_l = load_list("two_l", two)
         xs = load_scale_rows([nc.scalar, nc.sync, nc.scalar, nc.scalar], "xs", x_scales)
         offs_l = load_list("offs_l", offs)
+        w2w_raw = load_words(nc.sync, "w2w_raw", w2_words)
         xw = sb.tile([P, T], U32, name="xw", align_bytes=64)
-        nc.sync.dma_start(xw[:].bitcast(I32), x_words[0].rearrange("p n t -> p (n t)").bitcast(I32))
-        w2w_raw = load_words(nc.scalar, "w2w_raw", w2_words)
-        w1s_raw = load_scale_rows([nc.gpsimd] * 4, "w1s_raw", w1_scales)
-        w2s_raw = load_scale_rows([nc.scalar] * 4, "w2s_raw", w2_scales)
+        nc.scalar.dma_start(xw[:].bitcast(I32), x_words[0].rearrange("p n t -> p (n t)").bitcast(I32))
+        w2s_raw = load_scale_rows([nc.sync] * 4, "w2s_raw", w2_scales)
         w1w_raw = load_words(nc.sync, "w1w_raw", w1_words)
-        w3w_raw = load_words(nc.sync, "w3w_raw", w3_words)
-        w4w_raw = load_words(nc.sync, "w4w_raw", w4_words)
+        w1s_raw = load_scale_rows([nc.sync, nc.sync, nc.gpsimd, nc.gpsimd], "w1s_raw", w1_scales)
         gain = sb.tile([P, PACK], F32, name="gain")
         nc.sync.dma_start(gain[:], gn.rearrange("(p t) o -> p (t o)", t=PACK))
+        w3w_raw = load_words(nc.sync, "w3w_raw", w3_words)
         in2_l = load_list("in2_l", in2)
         in1_l = load_list("in1_l", in1)
         w3s_raw = load_scale_rows([nc.sync] * 4, "w3s_raw", w3_scales)
+        w4w_raw = load_words(nc.sync, "w4w_raw", w4_words)
         w4s_raw = load_scale_rows([nc.sync] * 4, "w4s_raw", w4_scales)
         mv_l = load_list("mv_l", mv)
         res_sb = sb.tile([P, PACK, S], F32, name="res_sb")
         nc.sync.dma_start(res_sb[:], res.rearrange("(p t) n -> p t n", t=PACK))
 
-        def pick(name, table, lst, dtype):
-            tl = sb.tile([P, S], dtype, name=name, align_bytes=64)
+        def pick(name, table, lst, dtype, tag=None):
+            tl = sb.tile([P, S], dtype, name=name, tag=tag or name, align_bytes=64)
             nc.vector.tensor_copy(tl[:], table[:].indirect(lst[:]))
             return tl
 
         two_s = pick("two_s", xs, two_l, U8)
         offs_s = pick("offs_s", xs, offs_l, U8)
         w2w = deal_words("w2w", w2w_raw)
-        w2s = deal_scales(nc.gpsimd, "w2s", w2s_raw)
-        two_w = pick("two_w", xw, two_l, U32)
+        w2s = deal_scales(nc.vector, "w2s", w2s_raw)
+        two_w = pick("two_w", xw, two_l, U32, "w2s_raw")
         w1w = deal_words("w1w", w1w_raw)
-        w1s = deal_scales(nc.gpsimd, "w1s", w1s_raw)
-        offs_w = pick("offs_w", xw, offs_l, U32)
+        w1s = deal_scales(nc.vector, "w1s", w1s_raw)
+        offs_w = pick("offs_w", xw, offs_l, U32, "w1s_raw")
 
         cap, push = [], []
         keep = sb.tile([P, PACK, S], F32, name="keep")
 
         def capacity(t):
-            pre = bank(t, 1, S)
+            pre = bank(C_BANKS[t], 1, S)
             product(pre[:, 0, :], w2w, w2s, t, two_w[:], two_s[:])
             c_t = sb.tile([P, S], F32, name="cap%d" % t)
             nc.scalar.activation(c_t[:], pre[:, 0, :], ACT.Sigmoid)
@@ -159,16 +161,8 @@ def tile_picked_pushflow_none_po_kernel(tc, x_words, x_scales, w1_words, w1_scal
                 kept(t - 1)
         kept(PACK - 1)
 
-        w3w = deal_word_bytes("w3w", w3w_raw)
-        w4w = deal_word_bytes("w4w", w4w_raw)
-        w3s = deal_scales(nc.gpsimd, "w3s", w3s_raw)
-        w4s = deal_scales(nc.gpsimd, "w4s", w4s_raw)
-        wide = END_CHUNKS[0][1]
-        gain_rows = []
-        for t in range(PACK if max(MOVE_ON_V) == PACK else 0):
-            gr = sb.tile([P, wide], F32, name="gain_row%d" % t)
-            nc.gpsimd.tensor_copy(gr[:], gain[:, t : t + 1].to_broadcast([P, wide]))
-            gain_rows.append(gr)
+        w3w = deal_word_bytes("w3w", w3w_raw, "w3w")
+        w3s = deal_scales(nc.vector, "w3s", w3s_raw)
 
         used = [0]
 
@@ -178,8 +172,8 @@ def tile_picked_pushflow_none_po_kernel(tc, x_words, x_scales, w1_words, w1_scal
 
         hid = [sb.tile([P, S], F32, name="hid%d" % t) for t in range(PACK)]
         for ci, (n0, n) in enumerate(MID_CHUNKS):
-            lost = sb.tile([P, PACK, n], F32, name="lost%d" % ci, tag=("pu3" if ci == 1 and HOLD_B else "lost%d" % ci))
-            gained = sb.tile([P, PACK, n], F32, name="gained%d" % ci)
+            lost = sb.tile([P, PACK, n], F32, name="lost%d" % ci, tag="lost%d" % ci, align_bytes=64)
+            gained = sb.tile([P, PACK, n], F32, name="gained%d" % ci, align_bytes=64)
             nv = GAIN_ON_V[ci]
             if nv < PACK:
                 got = sb.tile([P, PACK - nv, n], F32, name="got%d" % ci, tag=("got" if HOLD_B else "got%d" % ci))
@@ -210,6 +204,8 @@ def tile_picked_pushflow_none_po_kernel(tc, x_words, x_scales, w1_words, w1_scal
                     t = g0 + u
                     nc.scalar.activation(hid[t][:, n0 : n0 + n], acc[:, u, :], ACT.Tanh)
 
+        w4w = deal_word_bytes("w4w", w4w_raw, "gained1")
+        w4s = deal_scales(nc.vector, "w4s", w4s_raw, "lost1")
         out_rows = out_0.rearrange("(p t) n -> p t n", t=PACK)
         out_words = out_1[0].rearrange("p n t -> p (n t)").bitcast(I32)
         o_scales = sb.tile([P, S], U8, name="o_scales", align_bytes=64)
@@ -219,9 +215,7 @@ def tile_picked_pushflow_none_po_kernel(tc, x_words, x_scales, w1_words, w1_scal
             n0, n = END_CHUNKS[ci]
             mv_t = sb.tile([P, PACK, n], F32, name="moved%d" % ci, align_bytes=64)
             for t in range(PACK):
-                if MOVE_ON_V[ci] == PACK:
-                    nc.vector.tensor_tensor(mv_t[:, t, :], hid[t][:].indirect(cols(mv_l, n0, n)), gain_rows[t][:, :n], ALU.mult)
-                elif t < MOVE_ON_V[ci]:
+                if t < MOVE_ON_V[ci]:
                     nc.vector.tensor_copy(mv_t[:, t, :], hid[t][:].indirect(cols(mv_l, n0, n)))
                 else:
                     nc.scalar.activation(mv_t[:, t, :], hid[t][:].indirect(cols(mv_l, n0, n)), ACT.Copy)
@@ -230,11 +224,8 @@ def tile_picked_pushflow_none_po_kernel(tc, x_words, x_scales, w1_words, w1_scal
         def quantise(ci):
             n0, n = END_CHUNKS[ci]
             z2 = sb.tile([P, n, PACK], BF16, name="z2_%d" % ci, tag="z2_%d" % (ci % HOLD_Z2), align_bytes=64)
-            if MOVE_ON_V[ci] == PACK:
-                nc.vector.tensor_copy(woven(z2[:]), by_lines(moved[ci][:]))
-            else:
-                spread = gain[:].unsqueeze(1).unsqueeze(3).to_broadcast([P, n // 4, PACK, 4])
-                nc.vector.tensor_tensor(woven(z2[:]), by_lines(moved[ci][:]), spread, ALU.mult)
+            spread = gain[:].unsqueeze(1).unsqueeze(3).to_broadcast([P, n // 4, PACK, 4])
+            nc.vector.tensor_tensor(woven(z2[:]), by_lines(moved[ci][:]), spread, ALU.mult)
             zw = sb.tile([P, n], U32, name="z2w%d" % ci, align_bytes=64)
             zs = sb.tile([P, n], U8, name="z2s%d" % ci, align_bytes=64)
             nc.vector.quantize_mx(out=zw[:].bitcast(FP8X4), scales=zs[:], in_=z2[:].rearrange("p n t -> p (n t)"))
@@ -245,7 +236,7 @@ def tile_picked_pushflow_none_po_kernel(tc, x_words, x_scales, w1_words, w1_scal
         def multiply(ci):
             n0, n = END_CHUNKS[ci]
             zw, zs = zq[ci]
-            per = S // n
+            per = S // n if ci < len(END_CHUNKS) - 1 else LAST_PER
             accs[ci] = []
             for g0 in range(0, PACK, per):
                 acc = bank(next_bank(), per, n)

@@ -20,15 +20,18 @@ P = 128
 PACK = 4
 MID_CHUNKS = [(0, 256), (256, 256)]
 END_CHUNKS = [(0, 128), (128, 128), (256, 128), (384, 128)]
-PUSH_ENG = "S"
-GAIN_ON_V = [4,2]
+PUSH_ENG = "G"
+GAIN_ON_V = [2,2]
 GOT_FIRST = True
-C_BANKS = [0, 1, 2, 3]
+WALK = 2
+IL_ON_S = [0, 0, 0, 0]
+HG = "SV"
+C_BANKS = [0,1,2,0]
 LAST_PER = 2
 HOLD_B = True
 HOLD_Z = True
 HOLD_Z2 = 1
-MOVE_ON_V = [4, 0, 0, 0]
+MOVE_ON_V = [3,0,0,0]
 ROUND_ON_V = [0, 0, 0, 1]
 
 
@@ -78,11 +81,11 @@ def tile_picked_pushflow_none_po_kernel(tc, x_words, x_scales, w1_words, w1_scal
             nc.tensor.matmul_mx(out=out, lhsT=words[:, 2 * P * t : 2 * P * (t + 1)].bitcast(FP4X4), lhsT_scale=scales[:, P * t : P * (t + 1)],
                                 rhs=rhs.bitcast(FP8X4), rhs_scale=rhs_scale, start=True, stop=True)
 
-        def by_lines(ap):
-            return ap.rearrange("p t (c i) -> p c t i", i=4)
+        def by_lines(ap, i=4):
+            return ap.rearrange("p t (c i) -> p c t i", i=i)
 
-        def woven(ap):
-            return ap.rearrange("p (c i) t -> p c t i", i=4)
+        def woven(ap, i=4):
+            return ap.rearrange("p (c i) t -> p c t i", i=i)
 
         def cols(lst, n0, n):
             return lst[:, n0 // 16 : (n0 + n) // 16]
@@ -95,13 +98,13 @@ def tile_picked_pushflow_none_po_kernel(tc, x_words, x_scales, w1_words, w1_scal
         nc.scalar.dma_start(xw[:].bitcast(I32), x_words[0].rearrange("p n t -> p (n t)").bitcast(I32))
         w2s_raw = load_scale_rows([nc.sync] * 4, "w2s_raw", w2_scales)
         w1w_raw = load_words(nc.sync, "w1w_raw", w1_words)
-        w1s_raw = load_scale_rows([nc.sync, nc.sync, nc.gpsimd, nc.gpsimd], "w1s_raw", w1_scales)
+        w3w_raw = load_words(nc.sync, "w3w_raw", w3_words)
+        w1s_raw = load_scale_rows([nc.sync] * 4, "w1s_raw", w1_scales)
         gain = sb.tile([P, PACK], F32, name="gain")
         nc.sync.dma_start(gain[:], gn.rearrange("(p t) o -> p (t o)", t=PACK))
-        w3w_raw = load_words(nc.sync, "w3w_raw", w3_words)
+        w3s_raw = load_scale_rows([nc.sync] * 4, "w3s_raw", w3_scales)
         in2_l = load_list("in2_l", in2)
         in1_l = load_list("in1_l", in1)
-        w3s_raw = load_scale_rows([nc.sync] * 4, "w3s_raw", w3_scales)
         w4w_raw = load_words(nc.sync, "w4w_raw", w4_words)
         w4s_raw = load_scale_rows([nc.sync] * 4, "w4s_raw", w4_scales)
         mv_l = load_list("mv_l", mv)
@@ -116,11 +119,12 @@ def tile_picked_pushflow_none_po_kernel(tc, x_words, x_scales, w1_words, w1_scal
         two_s = pick("two_s", xs, two_l, U8)
         offs_s = pick("offs_s", xs, offs_l, U8)
         w2w = deal_words("w2w", w2w_raw)
+        two_w = pick("two_w", xw, two_l, U32)
         w2s = deal_scales(nc.vector, "w2s", w2s_raw)
-        two_w = pick("two_w", xw, two_l, U32, "w2s_raw")
         w1w = deal_words("w1w", w1w_raw)
+        w3w = deal_words("w3w", w3w_raw)
+        offs_w = pick("offs_w", xw, offs_l, U32, "w2s_raw")
         w1s = deal_scales(nc.vector, "w1s", w1s_raw)
-        offs_w = pick("offs_w", xw, offs_l, U32, "w1s_raw")
 
         cap, push = [], []
         keep = sb.tile([P, PACK, S], F32, name="keep")
@@ -137,7 +141,7 @@ def tile_picked_pushflow_none_po_kernel(tc, x_words, x_scales, w1_words, w1_scal
         def excess(t):
             y = bank(4 + t, 1, S)
             product(y[:, 0, :], w1w, w1s, t, offs_w[:], offs_s[:])
-            pu = sb.tile([P, S], F32, name="pu%d" % t)
+            pu = sb.tile([P, S], F32, name="pu%d" % t, align_bytes=64)
             nc.vector.scalar_tensor_tensor(pu[:], y[:, 0, :], 0.0, cap[t][:], ALU.max, ALU.min)
             pg = sb.tile([P, S], F32, name="push%d" % t)
             if PUSH_ENG == "S":
@@ -161,7 +165,6 @@ def tile_picked_pushflow_none_po_kernel(tc, x_words, x_scales, w1_words, w1_scal
                 kept(t - 1)
         kept(PACK - 1)
 
-        w3w = deal_word_bytes("w3w", w3w_raw, "w3w")
         w3s = deal_scales(nc.vector, "w3s", w3s_raw)
 
         used = [0]
@@ -171,8 +174,9 @@ def tile_picked_pushflow_none_po_kernel(tc, x_words, x_scales, w1_words, w1_scal
             return (len(used) - 2) % 8
 
         hid = [sb.tile([P, S], F32, name="hid%d" % t) for t in range(PACK)]
+        hg = [sb.tile([P, S], F32, name="hg%d" % t) for t in range(PACK)] if HG else hid
         for ci, (n0, n) in enumerate(MID_CHUNKS):
-            lost = sb.tile([P, PACK, n], F32, name="lost%d" % ci, tag="lost%d" % ci, align_bytes=64)
+            lost = sb.tile([P, PACK, n], F32, name="lost%d" % ci, tag="pu3" if ci == 1 else "lost%d" % ci, align_bytes=64)
             gained = sb.tile([P, PACK, n], F32, name="gained%d" % ci, align_bytes=64)
             nv = GAIN_ON_V[ci]
             if nv < PACK:
@@ -190,7 +194,7 @@ def tile_picked_pushflow_none_po_kernel(tc, x_words, x_scales, w1_words, w1_scal
             if nv < PACK:
                 nc.vector.tensor_tensor(gained[:, : PACK - nv, :], got[:], keep[:, : PACK - nv, n0 : n0 + n], ALU.add)
             z = sb.tile([P, n, PACK], BF16, name="z%d" % ci, tag="z" if HOLD_Z else "z%d" % ci, align_bytes=64)
-            nc.vector.tensor_tensor(woven(z[:]), by_lines(gained[:]), by_lines(lost[:]), ALU.add)
+            nc.vector.tensor_tensor(woven(z[:], WALK), by_lines(gained[:], WALK), by_lines(lost[:], WALK), ALU.add)
             zw = sb.tile([P, n], U32, name="zw%d" % ci, align_bytes=64)
             zs = sb.tile([P, n], U8, name="zs%d" % ci, align_bytes=64)
             nc.vector.quantize_mx(out=zw[:].bitcast(FP8X4), scales=zs[:], in_=z[:].rearrange("p n t -> p (n t)"))
@@ -203,9 +207,13 @@ def tile_picked_pushflow_none_po_kernel(tc, x_words, x_scales, w1_words, w1_scal
                 for u in range(per):
                     t = g0 + u
                     nc.scalar.activation(hid[t][:, n0 : n0 + n], acc[:, u, :], ACT.Tanh)
+                    if HG == "S" or (HG == "SV" and not last_mid):
+                        nc.scalar.activation(hg[t][:, n0 : n0 + n], hid[t][:, n0 : n0 + n], ACT.Copy, scale=gain[:, t : t + 1])
+                    elif HG:
+                        nc.vector.tensor_scalar(hg[t][:, n0 : n0 + n], hid[t][:, n0 : n0 + n], gain[:, t : t + 1], None, ALU.mult)
 
         w4w = deal_word_bytes("w4w", w4w_raw, "gained1")
-        w4s = deal_scales(nc.vector, "w4s", w4s_raw, "lost1")
+        w4s = deal_scales(nc.vector, "w4s", w4s_raw, "pu3")
         out_rows = out_0.rearrange("(p t) n -> p t n", t=PACK)
         out_words = out_1[0].rearrange("p n t -> p (n t)").bitcast(I32)
         o_scales = sb.tile([P, S], U8, name="o_scales", align_bytes=64)
@@ -216,16 +224,21 @@ def tile_picked_pushflow_none_po_kernel(tc, x_words, x_scales, w1_words, w1_scal
             mv_t = sb.tile([P, PACK, n], F32, name="moved%d" % ci, align_bytes=64)
             for t in range(PACK):
                 if t < MOVE_ON_V[ci]:
-                    nc.vector.tensor_copy(mv_t[:, t, :], hid[t][:].indirect(cols(mv_l, n0, n)))
+                    nc.vector.tensor_copy(mv_t[:, t, :], hg[t][:].indirect(cols(mv_l, n0, n)))
                 else:
-                    nc.scalar.activation(mv_t[:, t, :], hid[t][:].indirect(cols(mv_l, n0, n)), ACT.Copy)
+                    nc.scalar.activation(mv_t[:, t, :], hg[t][:].indirect(cols(mv_l, n0, n)), ACT.Copy)
             moved[ci] = mv_t
 
         def quantise(ci):
             n0, n = END_CHUNKS[ci]
             z2 = sb.tile([P, n, PACK], BF16, name="z2_%d" % ci, tag="z2_%d" % (ci % HOLD_Z2), align_bytes=64)
-            spread = gain[:].unsqueeze(1).unsqueeze(3).to_broadcast([P, n // 4, PACK, 4])
-            nc.vector.tensor_tensor(woven(z2[:]), by_lines(moved[ci][:]), spread, ALU.mult)
+            if HG and IL_ON_S[ci]:
+                nc.scalar.copy(woven(z2[:]), by_lines(moved[ci][:]))
+            elif HG:
+                nc.vector.tensor_copy(woven(z2[:]), by_lines(moved[ci][:]))
+            else:
+                spread = gain[:].unsqueeze(1).unsqueeze(3).to_broadcast([P, n // WALK, PACK, WALK])
+                nc.vector.tensor_tensor(woven(z2[:], WALK), by_lines(moved[ci][:], WALK), spread, ALU.mult)
             zw = sb.tile([P, n], U32, name="z2w%d" % ci, align_bytes=64)
             zs = sb.tile([P, n], U8, name="z2s%d" % ci, align_bytes=64)
             nc.vector.quantize_mx(out=zw[:].bitcast(FP8X4), scales=zs[:], in_=z2[:].rearrange("p n t -> p (n t)"))

@@ -20,18 +20,22 @@ P = 128
 PACK = 4
 MID_CHUNKS = [(0, 256), (256, 256)]
 END_CHUNKS = [(0, 128), (128, 128), (256, 128), (384, 128)]
-PUSH_ENG = "G"
-GAIN_ON_V = [2,2]
+PUSH_ENG = "S"
+GAIN_ON_V = [4,2]
 GOT_FIRST = True
-WALK = 2
-IL_ON_S = [0, 0, 0, 0]
+WALK = 4
+W4W_ON_S = False
+HOLD_Q0 = False
+W3W_ON_S = False
+WARM = False
+IL_ON_S = [0,0,0,0]
 HG = "SV"
-C_BANKS = [0,1,2,0]
+C_BANKS = [0,1,2,3]
 LAST_PER = 2
 HOLD_B = True
 HOLD_Z = True
-HOLD_Z2 = 1
-MOVE_ON_V = [3,0,0,0]
+HOLD_Z2 = 2
+MOVE_ON_V = [4,1,0,0]
 ROUND_ON_V = [0, 0, 0, 1]
 
 
@@ -59,8 +63,8 @@ def tile_picked_pushflow_none_po_kernel(tc, x_words, x_scales, w1_words, w1_scal
             queue.dma_start(tl[:].bitcast(I32), src[0].bitcast(I32))
             return tl
 
-        def deal_words(name, raw):
-            tl = sb.tile([P, 2 * H], U8, name=name, align_bytes=64)
+        def deal_words(name, raw, tag=None):
+            tl = sb.tile([P, 2 * H], U8, name=name, tag=tag or name, align_bytes=64)
             nc.scalar.copy(tl[:].bitcast(U16).rearrange("p (t m) -> p m t", t=PACK), raw[:].bitcast(U16).rearrange("p (m t) -> p m t", t=PACK))
             return tl
 
@@ -98,8 +102,8 @@ def tile_picked_pushflow_none_po_kernel(tc, x_words, x_scales, w1_words, w1_scal
         nc.scalar.dma_start(xw[:].bitcast(I32), x_words[0].rearrange("p n t -> p (n t)").bitcast(I32))
         w2s_raw = load_scale_rows([nc.sync] * 4, "w2s_raw", w2_scales)
         w1w_raw = load_words(nc.sync, "w1w_raw", w1_words)
-        w3w_raw = load_words(nc.sync, "w3w_raw", w3_words)
         w1s_raw = load_scale_rows([nc.sync] * 4, "w1s_raw", w1_scales)
+        w3w_raw = load_words(nc.sync, "w3w_raw", w3_words)
         gain = sb.tile([P, PACK], F32, name="gain")
         nc.sync.dma_start(gain[:], gn.rearrange("(p t) o -> p (t o)", t=PACK))
         w3s_raw = load_scale_rows([nc.sync] * 4, "w3s_raw", w3_scales)
@@ -110,6 +114,12 @@ def tile_picked_pushflow_none_po_kernel(tc, x_words, x_scales, w1_words, w1_scal
         mv_l = load_list("mv_l", mv)
         res_sb = sb.tile([P, PACK, S], F32, name="res_sb")
         nc.sync.dma_start(res_sb[:], res.rearrange("(p t) n -> p t n", t=PACK))
+
+        if WARM:
+            warm_in = sb.tile([P, 1], F32, name="warm_in")
+            warm_out = sb.tile([P, 1], F32, name="warm_out")
+            nc.vector.memset(warm_in[:], 0.0)
+            nc.scalar.activation(warm_out[:], warm_in[:], ACT.Sigmoid)
 
         def pick(name, table, lst, dtype, tag=None):
             tl = sb.tile([P, S], dtype, name=name, tag=tag or name, align_bytes=64)
@@ -122,7 +132,8 @@ def tile_picked_pushflow_none_po_kernel(tc, x_words, x_scales, w1_words, w1_scal
         two_w = pick("two_w", xw, two_l, U32)
         w2s = deal_scales(nc.vector, "w2s", w2s_raw)
         w1w = deal_words("w1w", w1w_raw)
-        w3w = deal_words("w3w", w3w_raw)
+        if W3W_ON_S:
+            w3w = deal_words("w3w", w3w_raw)
         offs_w = pick("offs_w", xw, offs_l, U32, "w2s_raw")
         w1s = deal_scales(nc.vector, "w1s", w1s_raw)
 
@@ -156,15 +167,16 @@ def tile_picked_pushflow_none_po_kernel(tc, x_words, x_scales, w1_words, w1_scal
         def kept(t):
             nc.vector.scalar_tensor_tensor(keep[:, t, :], ys[t][:, 0, :], gain[:, t : t + 1], push[t][:], ALU.mult, ALU.subtract)
 
-        capacity(0)
         for t in range(PACK):
-            if t + 1 < PACK:
-                capacity(t + 1)
+            capacity(t)
+        for t in range(PACK):
             excess(t)
             if t >= 1:
                 kept(t - 1)
         kept(PACK - 1)
 
+        if not W3W_ON_S:
+            w3w = deal_word_bytes("w3w", w3w_raw, "w1s_raw")
         w3s = deal_scales(nc.vector, "w3s", w3s_raw)
 
         used = [0]
@@ -177,7 +189,7 @@ def tile_picked_pushflow_none_po_kernel(tc, x_words, x_scales, w1_words, w1_scal
         hg = [sb.tile([P, S], F32, name="hg%d" % t) for t in range(PACK)] if HG else hid
         for ci, (n0, n) in enumerate(MID_CHUNKS):
             lost = sb.tile([P, PACK, n], F32, name="lost%d" % ci, tag="pu3" if ci == 1 else "lost%d" % ci, align_bytes=64)
-            gained = sb.tile([P, PACK, n], F32, name="gained%d" % ci, align_bytes=64)
+            gained = sb.tile([P, PACK, n], F32, name="gained%d" % ci, tag="gained%d" % ci, align_bytes=64)
             nv = GAIN_ON_V[ci]
             if nv < PACK:
                 got = sb.tile([P, PACK - nv, n], F32, name="got%d" % ci, tag=("got" if HOLD_B else "got%d" % ci))
@@ -193,7 +205,7 @@ def tile_picked_pushflow_none_po_kernel(tc, x_words, x_scales, w1_words, w1_scal
                     nc.scalar.activation(lost[:, t, :], push[t][:].indirect(cols(in2_l, n0, n)), ACT.Copy, scale=-0.5)
             if nv < PACK:
                 nc.vector.tensor_tensor(gained[:, : PACK - nv, :], got[:], keep[:, : PACK - nv, n0 : n0 + n], ALU.add)
-            z = sb.tile([P, n, PACK], BF16, name="z%d" % ci, tag="z" if HOLD_Z else "z%d" % ci, align_bytes=64)
+            z = sb.tile([P, n, PACK], BF16, name="z%d" % ci, tag="gained1" if (HOLD_Q0 and ci == 0) else "z%d" % ci, align_bytes=64)
             nc.vector.tensor_tensor(woven(z[:], WALK), by_lines(gained[:], WALK), by_lines(lost[:], WALK), ALU.add)
             zw = sb.tile([P, n], U32, name="zw%d" % ci, align_bytes=64)
             zs = sb.tile([P, n], U8, name="zs%d" % ci, align_bytes=64)
@@ -212,11 +224,12 @@ def tile_picked_pushflow_none_po_kernel(tc, x_words, x_scales, w1_words, w1_scal
                     elif HG:
                         nc.vector.tensor_scalar(hg[t][:, n0 : n0 + n], hid[t][:, n0 : n0 + n], gain[:, t : t + 1], None, ALU.mult)
 
-        w4w = deal_word_bytes("w4w", w4w_raw, "gained1")
+        w4w = deal_words("w4w", w4w_raw, "lost0") if W4W_ON_S else deal_word_bytes("w4w", w4w_raw, "gained1")
         w4s = deal_scales(nc.vector, "w4s", w4s_raw, "pu3")
         out_rows = out_0.rearrange("(p t) n -> p t n", t=PACK)
         out_words = out_1[0].rearrange("p n t -> p (n t)").bitcast(I32)
         o_scales = sb.tile([P, S], U8, name="o_scales", align_bytes=64)
+        o_words = sb.tile([P, S], U32, name="o_words", align_bytes=64)
         moved, zq = {}, {}
 
         def fetch(ci):
@@ -273,9 +286,10 @@ def tile_picked_pushflow_none_po_kernel(tc, x_words, x_scales, w1_words, w1_scal
                 nc.scalar.copy(woven(ob[:]), by_lines(o[:]))
             else:
                 nc.vector.tensor_copy(woven(ob[:]), by_lines(o[:]))
-            ow = sb.tile([P, n], U32, name="ow%d" % ci, align_bytes=64)
-            nc.vector.quantize_mx(out=ow[:].bitcast(FP8X4), scales=o_scales[:, n0 : n0 + n], in_=ob[:].rearrange("p n t -> p (n t)"))
-            nc.sync.dma_start(out_words[:, n0 : n0 + n], ow[:].bitcast(I32))
+            nc.vector.quantize_mx(out=o_words[:, n0 : n0 + n].bitcast(FP8X4), scales=o_scales[:, n0 : n0 + n], in_=ob[:].rearrange("p n t -> p (n t)"))
+            if ci % 2 == 1:
+                s0 = END_CHUNKS[ci - 1][0]
+                nc.sync.dma_start(out_words[:, s0 : n0 + n], o_words[:, s0 : n0 + n].bitcast(I32))
 
         for ci in range(len(END_CHUNKS)):
             fetch(ci)

from contextlib import ExitStack

import concourse.mybir as mybir

K, T, S, N, H = 512, 2048, 512, 512, 512
FLOPS = 4 * 2 * 512 * 512 * 512

F32 = mybir.dt.float32
BF16 = mybir.dt.bfloat16
I32 = mybir.dt.int32
U32 = mybir.dt.uint32
U16 = mybir.dt.uint16
U8 = mybir.dt.uint8
FP8X4 = mybir.dt.float8_e4m3fn_x4
FP4X4 = mybir.dt.float4_e2m1fn_x4
ALU = mybir.AluOpType
ACT = mybir.ActivationFunctionType

P = 128
PACK = 4
MID_CHUNKS = [(0, 256), (256, 256)]
END_CHUNKS = [(0, 128), (128, 128), (256, 128), (384, 128)]
PUSH_ENG = "S"
GAIN_ON_V = [4,2]
GOT_FIRST = True
WALK = 4
W4W_ON_S = False
HOLD_Q0 = False
W3W_ON_S = False
WARM = False
IL_ON_S = [0,0,0,0]
HG = "SV"
C_BANKS = [0,1,2,3]
LAST_PER = 2
HOLD_B = True
HOLD_Z = True
HOLD_Z2 = 2
MOVE_ON_V = [4,1,0,0]
ROUND_ON_V = [0, 0, 0, 1]


def tile_picked_pushflow_none_po_kernel(tc, x_words, x_scales, w1_words, w1_scales, w2_words, w2_scales, gn, w3_words, w3_scales, res, w4_words, w4_scales, offs, two, in1, in2, mv, out_0, out_1, out_2):
    nc = tc.nc
    with ExitStack() as ctx:
        lists = ctx.enter_context(tc.tile_pool(name="lists", bufs=1))
        sb = ctx.enter_context(tc.tile_pool(name="sb", bufs=1))
        psum = ctx.enter_context(tc.psum_pool(name="psum", bufs=1))

        def load_list(name, src):
            tl = lists.tile([P, S // 16], U16, name=name)
            nc.sync.dma_start(tl[:], src)
            return tl

        def load_scale_rows(queue, name, src):
            width = src.shape[2]
            tl = sb.tile([P, width], U8, name=name, tag=name, align_bytes=64)
            for q in range(4):
                queue[q].dma_start(tl[32 * q : 32 * q + 32, :].bitcast(I32), src[0, 4 * q : 4 * q + 4, :].bitcast(I32).partition_broadcast(8))
            return tl

        def load_words(queue, name, src):
            tl = sb.tile([P, 2 * H], U8, name=name, align_bytes=64)
            queue.dma_start(tl[:].bitcast(I32), src[0].bitcast(I32))
            return tl

        def deal_words(name, raw, tag=None):
            tl = sb.tile([P, 2 * H], U8, name=name, tag=tag or name, align_bytes=64)
            nc.scalar.copy(tl[:].bitcast(U16).rearrange("p (t m) -> p m t", t=PACK), raw[:].bitcast(U16).rearrange("p (m t) -> p m t", t=PACK))
            return tl

        def deal_word_bytes(name, raw, tag):
            tl = sb.tile([P, 2 * H], U8, name=name, tag=tag, align_bytes=64)
            nc.vector.tensor_copy(tl[:].rearrange("p (t m b) -> p t m b", t=PACK, b=2), raw[:].rearrange("p (m t b) -> p t m b", t=PACK, b=2))
            return tl

        def deal_scales(engine, name, raw, tag=None):
            tl = sb.tile([P, H], U8, name=name, tag=tag or name, align_bytes=64)
            engine.tensor_copy(tl[:].rearrange("p (t m) -> p t m", t=PACK), raw[:].rearrange("p (m t) -> p t m", t=PACK))
            return tl

        def bank(b, parts, width):
            return psum.tile([P, parts, width], F32, name="bank%d" % b, tag="bank%d" % b)

        def product(out, words, scales, t, rhs, rhs_scale):
            nc.tensor.matmul_mx(out=out, lhsT=words[:, 2 * P * t : 2 * P * (t + 1)].bitcast(FP4X4), lhsT_scale=scales[:, P * t : P * (t + 1)],
                                rhs=rhs.bitcast(FP8X4), rhs_scale=rhs_scale, start=True, stop=True)

        def by_lines(ap, i=4):
            return ap.rearrange("p t (c i) -> p c t i", i=i)

        def woven(ap, i=4):
            return ap.rearrange("p (c i) t -> p c t i", i=i)

        def cols(lst, n0, n):
            return lst[:, n0 // 16 : (n0 + n) // 16]

        two_l = load_list("two_l", two)
        xs = load_scale_rows([nc.scalar, nc.sync, nc.scalar, nc.scalar], "xs", x_scales)
        offs_l = load_list("offs_l", offs)
        w2w_raw = load_words(nc.sync, "w2w_raw", w2_words)
        xw = sb.tile([P, T], U32, name="xw", align_bytes=64)
        nc.scalar.dma_start(xw[:].bitcast(I32), x_words[0].rearrange("p n t -> p (n t)").bitcast(I32))
        w2s_raw = load_scale_rows([nc.sync] * 4, "w2s_raw", w2_scales)
        w1w_raw = load_words(nc.sync, "w1w_raw", w1_words)
        w1s_raw = load_scale_rows([nc.sync] * 4, "w1s_raw", w1_scales)
        w3w_raw = load_words(nc.sync, "w3w_raw", w3_words)
        gain = sb.tile([P, PACK], F32, name="gain")
        nc.sync.dma_start(gain[:], gn.rearrange("(p t) o -> p (t o)", t=PACK))
        w3s_raw = load_scale_rows([nc.sync] * 4, "w3s_raw", w3_scales)
        in2_l = load_list("in2_l", in2)
        in1_l = load_list("in1_l", in1)
        w4w_raw = load_words(nc.sync, "w4w_raw", w4_words)
        w4s_raw = load_scale_rows([nc.sync] * 4, "w4s_raw", w4_scales)
        mv_l = load_list("mv_l", mv)
        res_sb = sb.tile([P, PACK, S], F32, name="res_sb")
        nc.sync.dma_start(res_sb[:], res.rearrange("(p t) n -> p t n", t=PACK))

        if WARM:
            warm_in = sb.tile([P, 1], F32, name="warm_in")
            warm_out = sb.tile([P, 1], F32, name="warm_out")
            nc.vector.memset(warm_in[:], 0.0)
            nc.scalar.activation(warm_out[:], warm_in[:], ACT.Sigmoid)

        def pick(name, table, lst, dtype, tag=None):
            tl = sb.tile([P, S], dtype, name=name, tag=tag or name, align_bytes=64)
            nc.vector.tensor_copy(tl[:], table[:].indirect(lst[:]))
            return tl

        two_s = pick("two_s", xs, two_l, U8)
        offs_s = pick("offs_s", xs, offs_l, U8)
        w2w = deal_words("w2w", w2w_raw)
        two_w = pick("two_w", xw, two_l, U32)
        w2s = deal_scales(nc.vector, "w2s", w2s_raw)
        w1w = deal_words("w1w", w1w_raw)
        if W3W_ON_S:
            w3w = deal_words("w3w", w3w_raw)
        offs_w = pick("offs_w", xw, offs_l, U32, "w2s_raw")
        w1s = deal_scales(nc.vector, "w1s", w1s_raw)

        cap, push = [], []
        keep = sb.tile([P, PACK, S], F32, name="keep")

        def capacity(t):
            pre = bank(C_BANKS[t], 1, S)
            product(pre[:, 0, :], w2w, w2s, t, two_w[:], two_s[:])
            c_t = sb.tile([P, S], F32, name="cap%d" % t)
            nc.scalar.activation(c_t[:], pre[:, 0, :], ACT.Sigmoid)
            cap.append(c_t)

        ys = []

        def excess(t):
            y = bank(4 + t, 1, S)
            product(y[:, 0, :], w1w, w1s, t, offs_w[:], offs_s[:])
            pu = sb.tile([P, S], F32, name="pu%d" % t, align_bytes=64)
            nc.vector.scalar_tensor_tensor(pu[:], y[:, 0, :], 0.0, cap[t][:], ALU.max, ALU.min)
            pg = sb.tile([P, S], F32, name="push%d" % t)
            if PUSH_ENG == "S":
                nc.scalar.activation(pg[:], pu[:], ACT.Copy, scale=gain[:, t : t + 1])
            elif PUSH_ENG == "V":
                nc.vector.tensor_scalar(pg[:], pu[:], gain[:, t : t + 1], None, ALU.mult)
            else:
                nc.gpsimd.tensor_scalar(pg[:], pu[:], gain[:, t : t + 1], 0.0, ALU.mult, ALU.add)
            push.append(pg)
            ys.append(y)

        def kept(t):
            nc.vector.scalar_tensor_tensor(keep[:, t, :], ys[t][:, 0, :], gain[:, t : t + 1], push[t][:], ALU.mult, ALU.subtract)

        for t in range(PACK):
            capacity(t)
        for t in range(PACK):
            excess(t)
            if t >= 1:
                kept(t - 1)
        kept(PACK - 1)

        if not W3W_ON_S:
            w3w = deal_word_bytes("w3w", w3w_raw, "w1s_raw")
        w3s = deal_scales(nc.vector, "w3s", w3s_raw)

        used = [0]

        def next_bank():
            used.append(0)
            return (len(used) - 2) % 8

        hid = [sb.tile([P, S], F32, name="hid%d" % t) for t in range(PACK)]
        hg = [sb.tile([P, S], F32, name="hg%d" % t) for t in range(PACK)] if HG else hid
        for ci, (n0, n) in enumerate(MID_CHUNKS):
            lost = sb.tile([P, PACK, n], F32, name="lost%d" % ci, tag="pu3" if ci == 1 else "lost%d" % ci, align_bytes=64)
            gained = sb.tile([P, PACK, n], F32, name="gained%d" % ci, tag="gained%d" % ci, align_bytes=64)
            nv = GAIN_ON_V[ci]
            if nv < PACK:
                got = sb.tile([P, PACK - nv, n], F32, name="got%d" % ci, tag=("got" if HOLD_B else "got%d" % ci))
            for t in range(PACK):
                if not (GOT_FIRST and ci > 0):
                    nc.scalar.activation(lost[:, t, :], push[t][:].indirect(cols(in2_l, n0, n)), ACT.Copy, scale=-0.5)
                if t >= PACK - nv:
                    nc.vector.tensor_tensor(gained[:, t, :], push[t][:].indirect(cols(in1_l, n0, n)), keep[:, t, n0 : n0 + n], ALU.add)
                else:
                    nc.scalar.activation(got[:, t, :], push[t][:].indirect(cols(in1_l, n0, n)), ACT.Copy)
            for t in range(PACK):
                if GOT_FIRST and ci > 0:
                    nc.scalar.activation(lost[:, t, :], push[t][:].indirect(cols(in2_l, n0, n)), ACT.Copy, scale=-0.5)
            if nv < PACK:
                nc.vector.tensor_tensor(gained[:, : PACK - nv, :], got[:], keep[:, : PACK - nv, n0 : n0 + n], ALU.add)
            z = sb.tile([P, n, PACK], BF16, name="z%d" % ci, tag="gained1" if (HOLD_Q0 and ci == 0) else "z%d" % ci, align_bytes=64)
            nc.vector.tensor_tensor(woven(z[:], WALK), by_lines(gained[:], WALK), by_lines(lost[:], WALK), ALU.add)
            zw = sb.tile([P, n], U32, name="zw%d" % ci, align_bytes=64)
            zs = sb.tile([P, n], U8, name="zs%d" % ci, align_bytes=64)
            nc.vector.quantize_mx(out=zw[:].bitcast(FP8X4), scales=zs[:], in_=z[:].rearrange("p n t -> p (n t)"))
            last_mid = ci == len(MID_CHUNKS) - 1
            per = 1 if last_mid else S // n
            for g0 in range(0, PACK, per):
                acc = bank(next_bank(), per, n)
                for u in range(per):
                    product(acc[:, u, :], w3w, w3s, g0 + u, zw[:], zs[:])
                for u in range(per):
                    t = g0 + u
                    nc.scalar.activation(hid[t][:, n0 : n0 + n], acc[:, u, :], ACT.Tanh)
                    if HG == "S" or (HG == "SV" and not last_mid):
                        nc.scalar.activation(hg[t][:, n0 : n0 + n], hid[t][:, n0 : n0 + n], ACT.Copy, scale=gain[:, t : t + 1])
                    elif HG:
                        nc.vector.tensor_scalar(hg[t][:, n0 : n0 + n], hid[t][:, n0 : n0 + n], gain[:, t : t + 1], None, ALU.mult)

        w4w = deal_words("w4w", w4w_raw, "lost0") if W4W_ON_S else deal_word_bytes("w4w", w4w_raw, "gained1")
        w4s = deal_scales(nc.vector, "w4s", w4s_raw, "pu3")
        out_rows = out_0.rearrange("(p t) n -> p t n", t=PACK)
        out_words = out_1[0].rearrange("p n t -> p (n t)").bitcast(I32)
        o_scales = sb.tile([P, S], U8, name="o_scales", align_bytes=64)
        o_words = sb.tile([P, S], U32, name="o_words", align_bytes=64)
        moved, zq = {}, {}

        def fetch(ci):
            n0, n = END_CHUNKS[ci]
            mv_t = sb.tile([P, PACK, n], F32, name="moved%d" % ci, align_bytes=64)
            for t in range(PACK):
                if t < MOVE_ON_V[ci]:
                    nc.vector.tensor_copy(mv_t[:, t, :], hg[t][:].indirect(cols(mv_l, n0, n)))
                else:
                    nc.scalar.activation(mv_t[:, t, :], hg[t][:].indirect(cols(mv_l, n0, n)), ACT.Copy)
            moved[ci] = mv_t

        def quantise(ci):
            n0, n = END_CHUNKS[ci]
            z2 = sb.tile([P, n, PACK], BF16, name="z2_%d" % ci, tag="z2_%d" % (ci % HOLD_Z2), align_bytes=64)
            if HG and IL_ON_S[ci]:
                nc.scalar.copy(woven(z2[:]), by_lines(moved[ci][:]))
            elif HG:
                nc.vector.tensor_copy(woven(z2[:]), by_lines(moved[ci][:]))
            else:
                spread = gain[:].unsqueeze(1).unsqueeze(3).to_broadcast([P, n // WALK, PACK, WALK])
                nc.vector.tensor_tensor(woven(z2[:], WALK), by_lines(moved[ci][:], WALK), spread, ALU.mult)
            zw = sb.tile([P, n], U32, name="z2w%d" % ci, align_bytes=64)
            zs = sb.tile([P, n], U8, name="z2s%d" % ci, align_bytes=64)
            nc.vector.quantize_mx(out=zw[:].bitcast(FP8X4), scales=zs[:], in_=z2[:].rearrange("p n t -> p (n t)"))
            zq[ci] = (zw, zs)

        accs, outs = {}, {}

        def multiply(ci):
            n0, n = END_CHUNKS[ci]
            zw, zs = zq[ci]
            per = S // n if ci < len(END_CHUNKS) - 1 else LAST_PER
            accs[ci] = []
            for g0 in range(0, PACK, per):
                acc = bank(next_bank(), per, n)
                for u in range(per):
                    product(acc[:, u, :], w4w, w4s, g0 + u, zw[:], zs[:])
                accs[ci].append((g0, per, acc))

        def finish(ci):
            n0, n = END_CHUNKS[ci]
            o = sb.tile([P, PACK, n], F32, name="o%d" % ci)
            for g0, per, acc in accs[ci]:
                nc.vector.tensor_tensor(o[:, g0 : g0 + per, :], acc[:], res_sb[:, g0 : g0 + per, n0 : n0 + n], ALU.add)
            nc.sync.dma_start(out_rows[:, :, n0 : n0 + n], o[:])
            outs[ci] = o

        def planes(ci):
            n0, n = END_CHUNKS[ci]
            o = outs[ci]
            ob = sb.tile([P, n, PACK], BF16, name="ob%d" % ci, align_bytes=64)
            if not ROUND_ON_V[ci]:
                nc.scalar.copy(woven(ob[:]), by_lines(o[:]))
            else:
                nc.vector.tensor_copy(woven(ob[:]), by_lines(o[:]))
            nc.vector.quantize_mx(out=o_words[:, n0 : n0 + n].bitcast(FP8X4), scales=o_scales[:, n0 : n0 + n], in_=ob[:].rearrange("p n t -> p (n t)"))
            if ci % 2 == 1:
                s0 = END_CHUNKS[ci - 1][0]
                nc.sync.dma_start(out_words[:, s0 : n0 + n], o_words[:, s0 : n0 + n].bitcast(I32))

        for ci in range(len(END_CHUNKS)):
            fetch(ci)
            quantise(ci)
            multiply(ci)
        for ci in range(len(END_CHUNKS)):
            finish(ci)
        for ci in range(len(END_CHUNKS)):
            planes(ci)
        for q in range(4):
            (nc.scalar if q % 2 == 0 else nc.sync).dma_start(out_2[0, 4 * q : 4 * q + 4, :].bitcast(I32), o_scales[32 * q : 32 * q + 4, :].bitcast(I32))
